import numpy as np, ml_dtypes
CORES = [2,3,6,7,58,59,62,63,114,115,118,119]
N = 12
QP = 32
def setup_inputs(rng):
    return {"q": rng.standard_normal((N, 128, QP), dtype=np.float32).astype(ml_dtypes.bfloat16), "k": rng.standard_normal((N, 128, 128), dtype=np.float32).astype(ml_dtypes.bfloat16), "v": rng.standard_normal((N, 128, 128), dtype=np.float32).astype(ml_dtypes.bfloat16), "b": (8 * rng.standard_normal((N, 128, N * QP), dtype=np.float32)).astype(ml_dtypes.bfloat16)}
def setup_inputs_big(rng):
    d = setup_inputs(rng)
    for k in ("q", "k", "v", "b"): d[k] = (d[k].astype(np.float32) * 1024.0).astype(d[k].dtype)
    return d
def setup_inputs_small(rng):
    d = setup_inputs(rng)
    for k in ("q", "k", "v", "b"): d[k] = (d[k].astype(np.float32) * (1 / 1024.0)).astype(d[k].dtype)
    return d
def setup_inputs_apart(rng):
    d = setup_inputs(rng)
    f = (10.0 ** rng.permutation(np.linspace(-1.5, 1.5, N))).astype(np.float32).reshape(N, 1, 1)
    for k in ("q", "k", "v", "b"): d[k] = (d[k].astype(np.float32) * f).astype(d[k].dtype)
    return d
def reference(q, k, v, b):
    Q, K, V, B = q.astype(np.float64), k.astype(np.float64), v.astype(np.float64), b.astype(np.float64)
    y = np.zeros((N, 128, QP))
    for r in range(N):
        for j in range(N):
            y[r] += V[j].T @ np.maximum(K[j].T @ Q[r] + B[r][:, QP * j:QP * j + QP], 0.0)
    return {"y": y.astype(ml_dtypes.bfloat16 if q.dtype != np.float64 else np.float64)}

@@ -1,0 +1,161 @@
+from concourse.bass import DstId, RemoteDMATransfer
+from concourse.mybir import AluOpType
+
+NCH = 3
+NPC = 4
+QP = 32
+
+SCRATCH = {
+    "kva": ("sbuf", [128, NCH, 256], "bfloat16"),
+    "qs": ("sbuf", [128, QP], "bfloat16"),
+    "zero": ("sbuf", [128, QP], "bfloat16"),
+    "bs": ("sbuf", [128, NCH, NPC, QP], "bfloat16"),
+    "win": ("sbuf", [128, NPC, 1 + NCH, QP], "bfloat16"),
+    "lq": ("sbuf", [128, NPC, 1 + NCH, QP], "bfloat16"),
+    "m": ("sbuf", [128, NCH, NPC, QP], "bfloat16"),
+    "asb": ("sbuf", [128, NPC, QP], "float32"),
+    "ob": ("sbuf", [128, NPC, QP], "bfloat16"),
+    "lo": ("sbuf", [128, NPC, QP], "bfloat16"),
+    "t": ("sbuf", [128, 2, QP], "float32"),
+    "ys": ("sbuf", [128, QP], "bfloat16"),
+    "p0": ("psum", [128, 16, QP], "float32"),
+    "p1": ("psum", [128, 16, QP], "float32"),
+    "p2": ("psum", [128, 16, QP], "float32"),
+    "pa": ("psum", [128, 16, QP], "float32"),
+    "pm": ("psum", [128, 16, QP], "float32"),
+}
+SEMAPHORES = ["ldkv", "ldq", "ldb", "vz", "cmpw", "cmpo", "kvin0", "kvin1", "kvin2", "qbin",
+              "sp0", "sp1", "sp2", "sm0", "sm1", "sm2", "sa", "sasb", "smm", "so", "oin", "st", "sy", "sty", "sent"]
+
+
+def _bits(mask):
+    return [e for e in range(mask.bit_length()) if (mask >> e) & 1]
+
+
+def _mask(bits):
+    m = 0
+    for e in bits:
+        m |= 1 << e
+    return m
+
+
+def rank_program(g, core, T, topo):
+    rank = T.rank_of(core)
+    if rank is None:
+        return
+    S = T.sem
+    cores = list(T.cores)
+    chips = []
+    for c in cores:
+        if topo.chip(c) not in chips:
+            chips.append(topo.chip(c))
+    groups = [[c for c in cores if topo.chip(c) == ch] for ch in chips]
+    ci = chips.index(topo.chip(core))
+    oi = groups[ci].index(core)
+    assert len(chips) == NCH and all(len(gr) == NPC for gr in groups) and rank == ci * NPC + oi
+
+    def dst_id(c):
+        rid, pid, _ = topo.addr(c)
+        return DstId(rid=rid, pnc=pid)
+
+    far = [groups[(ci + 1) % NCH][oi], groups[(ci + 2) % NCH][oi]]
+    for c in far:
+        assert topo.may_write(core, c) and topo.die(c) == topo.die(core)
+    ca, cb = (ci - 1) % NCH, (ci + 1) % NCH
+    mates = [o for o in range(NPC) if o != oi]
+
+    off = _bits(topo.mask(core, far[0]) & topo.mask(core, far[1]))
+    stay = [e for e in _bits(topo.mask(core, groups[ci][mates[0]])) if e not in off]
+    nw = 1
+    while nw * 2 * len(mates) <= len(stay):
+        nw *= 2
+    wmask = [stay[i * nw:(i + 1) * nw] for i in range(len(mates))]
+    used = off + [e for w in wmask for e in w]
+    no = 1
+    while no * 2 * len(mates) <= len(used):
+        no *= 2
+    omask = [used[i * no:(i + 1) * no] for i in range(len(mates))]
+
+    P = [T.p0, T.p1, T.p2]
+    sp = [S.sp0, S.sp1, S.sp2]
+    sm = [S.sm0, S.sm1, S.sm2]
+    kvin = [S.kvin0, S.kvin1, S.kvin2]
+
+    g.sync.dma_start(T.kva[:, ci, 0:128], T.k[:, :]).then_inc(S.ldkv, 16)
+    g.scalar.dma_start(T.kva[:, ci, 128:256], T.v[:, :]).then_inc(S.ldkv, 16)
+    g.sync.dma_start(T.qs[:, :], T.q[:, :]).then_inc(S.ldq, 16)
+    g.scalar.dma_start(T.bs[:, :, :, :], T.b[:, :]).then_inc(S.ldb, 16)
+
+    g.wait_ge(S.ldkv, 32)
+    g.remote_dma_fused([RemoteDMATransfer(
+        dst_ids=[dst_id(c) for c in far], dma_engine_mask=_mask(off), remote_sem=kvin[ci],
+        srcs=[T.kva[:, ci, :]], dsts=[T.kva[:, ci, :] for _ in far])], local_sem=S.sent)
+    g.wait_ge(S.cmpw, 2 * len(mates))
+    g.remote_dma_fused([RemoteDMATransfer(
+        dst_ids=[dst_id(groups[ci][o])], dma_engine_mask=_mask(wmask[i]), remote_sem=S.qbin,
+        src=T.win[:, o, :, :], dst=T.lq[:, oi, :, :]) for i, o in enumerate(mates)], local_sem=S.sent)
+    g.wait_ge(S.so, 1)
+    g.remote_dma_fused([RemoteDMATransfer(
+        dst_ids=[dst_id(groups[ci][o])], dma_engine_mask=_mask(omask[i]), remote_sem=S.oin,
+        src=T.ob[:, o, :], dst=T.lo[:, oi, :]) for i, o in enumerate(mates)], local_sem=S.sent)
+    g.wait_ge(S.sent, len(off) + len(mates) * (nw + no))
+
+    V = g.vector
+    V.memset(T.zero[:, :], 0.0).then_inc(S.vz, 1)
+    V.wait_ge(S.vz, 1)
+    V.wait_ge(S.ldq, 16)
+    for o in mates:
+        V.tensor_tensor(out=T.win[:, o, 0, :], in0=T.zero[:, :], in1=T.qs[:, :], op=AluOpType.subtract).then_inc(S.cmpw, 1)
+    V.tensor_tensor(out=T.lq[:, oi, 0, :], in0=T.zero[:, :], in1=T.qs[:, :], op=AluOpType.subtract).then_inc(S.cmpo, 1)
+    V.wait_ge(S.ldb, 16)
+    for o in mates:
+        V.tensor_copy(out=T.win[:, o, 1:1 + NCH, :], in_=T.bs[:, :, o, :]).then_inc(S.cmpw, 1)
+    V.tensor_copy(out=T.lq[:, oi, 1:1 + NCH, :], in_=T.bs[:, :, oi, :]).then_inc(S.cmpo, 1)
+    V.wait_ge(S.cmpo, 2)
+    V.wait_ge(S.qbin, nw * len(mates))
+    for c in (ci, ca, cb):
+        V.wait_ge(sp[c], 1)
+        V.tensor_tensor(out=T.m[:, c, :, :], in0=P[c][:, 0:NPC, :], in1=T.lq[:, :, 1 + c, :],
+                        op=AluOpType.min).then_inc(sm[c], 1)
+    V.wait_ge(S.sa, 1)
+    V.tensor_copy(out=T.asb[:, :, :], in_=T.pa[:, 0:NPC, :]).then_inc(S.sasb, 1)
+    V.wait_ge(S.sasb, 1)
+    V.wait_ge(S.smm, 1)
+    V.tensor_tensor(out=T.ob[:, :, :], in0=T.asb[:, :, :], in1=T.pm[:, 0:NPC, :], op=AluOpType.subtract).then_inc(S.so, 1)
+    V.wait_ge(S.so, 1)
+    V.wait_ge(S.oin, no * len(mates))
+    V.tensor_tensor(out=T.t[:, 0, :], in0=T.lo[:, mates[0], :], in1=T.lo[:, mates[1], :], op=AluOpType.add).then_inc(S.st, 1)
+    V.tensor_tensor(out=T.t[:, 1, :], in0=T.lo[:, mates[2], :], in1=T.ob[:, oi, :], op=AluOpType.add).then_inc(S.st, 1)
+    V.wait_ge(S.st, 2)
+    V.tensor_tensor(out=T.ys[:, :], in0=T.t[:, 0, :], in1=T.t[:, 1, :], op=AluOpType.add).then_inc(S.sy, 1)
+
+    E = g.tensor
+
+    def kk(c):
+        return T.kva[:, c, 0:128]
+
+    def vv(c):
+        return T.kva[:, c, 128:256]
+
+    nq = T.lq[:, :, 0, :]
+    E.wait_ge(S.ldkv, 32)
+    E.wait_ge(S.cmpo, 2)
+    E.wait_ge(S.qbin, nw * len(mates))
+    E.matmul(out=P[ci][:, 0:NPC, :], lhsT=kk(ci), rhs=nq, start=True, stop=True).then_inc(sp[ci], 1)
+    E.matmul(out=T.pa[:, 0:NPC, :], lhsT=vv(ci), rhs=T.lq[:, :, 1 + ci, :], start=True, stop=False)
+    E.wait_ge(kvin[ca], len(off))
+    E.matmul(out=P[ca][:, 0:NPC, :], lhsT=kk(ca), rhs=nq, start=True, stop=True).then_inc(sp[ca], 1)
+    E.matmul(out=T.pa[:, 0:NPC, :], lhsT=vv(ca), rhs=T.lq[:, :, 1 + ca, :], start=False, stop=False)
+    E.wait_ge(sm[ci], 1)
+    E.matmul(out=T.pm[:, 0:NPC, :], lhsT=vv(ci), rhs=T.m[:, ci, :, :], start=True, stop=False)
+    E.wait_ge(kvin[cb], len(off))
+    E.matmul(out=P[cb][:, 0:NPC, :], lhsT=kk(cb), rhs=nq, start=True, stop=True).then_inc(sp[cb], 1)
+    E.matmul(out=T.pa[:, 0:NPC, :], lhsT=vv(cb), rhs=T.lq[:, :, 1 + cb, :], start=False, stop=True).then_inc(S.sa, 1)
+    E.wait_ge(sm[ca], 1)
+    E.matmul(out=T.pm[:, 0:NPC, :], lhsT=vv(ca), rhs=T.m[:, ca, :, :], start=False, stop=False)
+    E.wait_ge(sm[cb], 1)
+    E.matmul(out=T.pm[:, 0:NPC, :], lhsT=vv(cb), rhs=T.m[:, cb, :, :], start=False, stop=True).then_inc(S.smm, 1)
+
+    g.sync.wait_ge(S.sy, 1)
+    g.sync.dma_start(T.y[:, :], T.ys[:, :]).then_inc(S.sty, 16)
+    g.sync.wait_ge(S.sty, 16)

@@ -6,14 +6,17 @@ NPC = 4
 QP = 32
 
 SCRATCH = {
-    "kva": ("sbuf", [128, NCH, 256], "bfloat16"),
+    "ka": ("sbuf", [128, NCH, 128], "bfloat16"),
+    "va": ("sbuf", [128, NCH, 128], "bfloat16"),
     "qs": ("sbuf", [128, QP], "bfloat16"),
-    "zero": ("sbuf", [128, QP], "bfloat16"),
+    "zero": ("sbuf", [128, NPC, QP], "bfloat16"),
+    "z": ("sbuf", [128, 129], "bfloat16"),
+    "zd": ("dram", [1, 128 * 129], "bfloat16"),
+    "idn": ("sbuf", [128, 128], "bfloat16"),
     "bs": ("sbuf", [128, NCH, NPC, QP], "bfloat16"),
     "win": ("sbuf", [128, NPC, 1 + NCH, QP], "bfloat16"),
     "lq": ("sbuf", [128, NPC, 1 + NCH, QP], "bfloat16"),
-    "m": ("sbuf", [128, NCH, NPC, QP], "bfloat16"),
-    "asb": ("sbuf", [128, NPC, QP], "float32"),
+    "s": ("sbuf", [128, NCH, NPC, QP], "bfloat16"),
     "ob": ("sbuf", [128, NPC, QP], "bfloat16"),
     "lo": ("sbuf", [128, NPC, QP], "bfloat16"),
     "t": ("sbuf", [128, 2, QP], "float32"),
@@ -21,11 +24,10 @@ SCRATCH = {
     "p0": ("psum", [128, 16, QP], "float32"),
     "p1": ("psum", [128, 16, QP], "float32"),
     "p2": ("psum", [128, 16, QP], "float32"),
-    "pa": ("psum", [128, 16, QP], "float32"),
-    "pm": ("psum", [128, 16, QP], "float32"),
+    "po": ("psum", [128, 16, QP], "float32"),
 }
-SEMAPHORES = ["ldkv", "ldq", "ldb", "vz", "cmpw", "cmpo", "kvin0", "kvin1", "kvin2", "qbin",
-              "sp0", "sp1", "sp2", "sm0", "sm1", "sm2", "sa", "sasb", "smm", "so", "oin", "st", "sy", "sty", "sent"]
+SEMAPHORES = ["ldk", "ldv", "ldq", "ldb", "vz", "vid", "sd1", "sid", "cmpw", "cmpo", "kin0", "kin1", "kin2", "vin0", "vin1",
+              "vin2", "qbin", "sp0", "sp1", "sp2", "ss0", "ss1", "ss2", "spo", "so", "oin", "st", "sy", "sty", "sent"]
 
 
 def _bits(mask):
@@ -78,50 +80,54 @@ def rank_program(g, core, T, topo):
 
     P = [T.p0, T.p1, T.p2]
     sp = [S.sp0, S.sp1, S.sp2]
-    sm = [S.sm0, S.sm1, S.sm2]
-    kvin = [S.kvin0, S.kvin1, S.kvin2]
+    ss = [S.ss0, S.ss1, S.ss2]
+    kin = [S.kin0, S.kin1, S.kin2]
+    vin = [S.vin0, S.vin1, S.vin2]
 
-    g.sync.dma_start(T.kva[:, ci, 0:128], T.k[:, :]).then_inc(S.ldkv, 16)
-    g.scalar.dma_start(T.kva[:, ci, 128:256], T.v[:, :]).then_inc(S.ldkv, 16)
+    g.sync.dma_start(T.ka[:, ci, :], T.k[:, :]).then_inc(S.ldk, 16)
+    g.scalar.dma_start(T.va[:, ci, :], T.v[:, :]).then_inc(S.ldv, 16)
     g.sync.dma_start(T.qs[:, :], T.q[:, :]).then_inc(S.ldq, 16)
     g.scalar.dma_start(T.bs[:, :, :, :], T.b[:, :]).then_inc(S.ldb, 16)
+    g.sync.wait_ge(S.vid, 2)
+    g.sync.dma_start(T.zd[0:1, :], T.z[:, :]).then_inc(S.sd1, 16)
+    g.sync.wait_ge(S.sd1, 16)
+    g.sync.dma_start(T.idn[:, :], T.zd[0:1, 0:128 * 128]).then_inc(S.sid, 16)
 
-    g.wait_ge(S.ldkv, 32)
+    g.wait_ge(S.ldk, 16)
     g.remote_dma_fused([RemoteDMATransfer(
-        dst_ids=[dst_id(c) for c in far], dma_engine_mask=_mask(off), remote_sem=kvin[ci],
-        srcs=[T.kva[:, ci, :]], dsts=[T.kva[:, ci, :] for _ in far])], local_sem=S.sent)
+        dst_ids=[dst_id(c) for c in far], dma_engine_mask=_mask(off), remote_sem=kin[ci],
+        srcs=[T.ka[:, ci, :]], dsts=[T.ka[:, ci, :] for _ in far])], local_sem=S.sent)
+    g.wait_ge(S.ldv, 16)
     g.wait_ge(S.cmpw, 2 * len(mates))
     g.remote_dma_fused([RemoteDMATransfer(
-        dst_ids=[dst_id(groups[ci][o])], dma_engine_mask=_mask(wmask[i]), remote_sem=S.qbin,
-        src=T.win[:, o, :, :], dst=T.lq[:, oi, :, :]) for i, o in enumerate(mates)], local_sem=S.sent)
+        dst_ids=[dst_id(c) for c in far], dma_engine_mask=_mask(off), remote_sem=vin[ci],
+        srcs=[T.va[:, ci, :]], dsts=[T.va[:, ci, :] for _ in far])] + [RemoteDMATransfer(
+            dst_ids=[dst_id(groups[ci][o])], dma_engine_mask=_mask(wmask[i]), remote_sem=S.qbin,
+            src=T.win[:, o, :, :], dst=T.lq[:, oi, :, :]) for i, o in enumerate(mates)], local_sem=S.sent)
     g.wait_ge(S.so, 1)
     g.remote_dma_fused([RemoteDMATransfer(
         dst_ids=[dst_id(groups[ci][o])], dma_engine_mask=_mask(omask[i]), remote_sem=S.oin,
         src=T.ob[:, o, :], dst=T.lo[:, oi, :]) for i, o in enumerate(mates)], local_sem=S.sent)
-    g.wait_ge(S.sent, len(off) + len(mates) * (nw + no))
+    g.wait_ge(S.sent, 2 * len(off) + len(mates) * (nw + no))
 
     V = g.vector
-    V.memset(T.zero[:, :], 0.0).then_inc(S.vz, 1)
-    V.wait_ge(S.vz, 1)
+    V.memset(T.z[:, 0:1], 1.0).then_inc(S.vid, 1)
+    V.memset(T.z[:, 1:129], 0.0).then_inc(S.vid, 1)
+    V.memset(T.zero[:, :, :], 0.0).then_inc(S.vz, 1)
     V.wait_ge(S.ldq, 16)
     for o in mates:
-        V.tensor_tensor(out=T.win[:, o, 0, :], in0=T.zero[:, :], in1=T.qs[:, :], op=AluOpType.subtract).then_inc(S.cmpw, 1)
-    V.tensor_tensor(out=T.lq[:, oi, 0, :], in0=T.zero[:, :], in1=T.qs[:, :], op=AluOpType.subtract).then_inc(S.cmpo, 1)
+        V.tensor_copy(out=T.win[:, o, 0, :], in_=T.qs[:, :]).then_inc(S.cmpw, 1)
+    V.tensor_copy(out=T.lq[:, oi, 0, :], in_=T.qs[:, :]).then_inc(S.cmpo, 1)
     V.wait_ge(S.ldb, 16)
     for o in mates:
         V.tensor_copy(out=T.win[:, o, 1:1 + NCH, :], in_=T.bs[:, :, o, :]).then_inc(S.cmpw, 1)
     V.tensor_copy(out=T.lq[:, oi, 1:1 + NCH, :], in_=T.bs[:, :, oi, :]).then_inc(S.cmpo, 1)
-    V.wait_ge(S.cmpo, 2)
-    V.wait_ge(S.qbin, nw * len(mates))
+    V.wait_ge(S.vz, 1)
     for c in (ci, ca, cb):
         V.wait_ge(sp[c], 1)
-        V.tensor_tensor(out=T.m[:, c, :, :], in0=P[c][:, 0:NPC, :], in1=T.lq[:, :, 1 + c, :],
-                        op=AluOpType.min).then_inc(sm[c], 1)
-    V.wait_ge(S.sa, 1)
-    V.tensor_copy(out=T.asb[:, :, :], in_=T.pa[:, 0:NPC, :]).then_inc(S.sasb, 1)
-    V.wait_ge(S.sasb, 1)
-    V.wait_ge(S.smm, 1)
-    V.tensor_tensor(out=T.ob[:, :, :], in0=T.asb[:, :, :], in1=T.pm[:, 0:NPC, :], op=AluOpType.subtract).then_inc(S.so, 1)
+        V.tensor_tensor(out=T.s[:, c, :, :], in0=P[c][:, 0:NPC, :], in1=T.zero[:, :, :], op=AluOpType.max).then_inc(ss[c], 1)
+    V.wait_ge(S.spo, 1)
+    V.tensor_copy(out=T.ob[:, :, :], in_=T.po[:, 0:NPC, :]).then_inc(S.so, 1)
     V.wait_ge(S.so, 1)
     V.wait_ge(S.oin, no * len(mates))
     V.tensor_tensor(out=T.t[:, 0, :], in0=T.lo[:, mates[0], :], in1=T.lo[:, mates[1], :], op=AluOpType.add).then_inc(S.st, 1)
@@ -130,31 +136,35 @@ def rank_program(g, core, T, topo):
     V.tensor_tensor(out=T.ys[:, :], in0=T.t[:, 0, :], in1=T.t[:, 1, :], op=AluOpType.add).then_inc(S.sy, 1)
 
     E = g.tensor
+    qa = T.lq[:, :, 0, :]
 
-    def kk(c):
-        return T.kva[:, c, 0:128]
+    def addb(c):
+        E.matmul(out=P[c][:, 0:NPC, :], lhsT=T.idn[:, :], rhs=T.lq[:, :, 1 + c, :], start=True, stop=False)
 
-    def vv(c):
-        return T.kva[:, c, 128:256]
+    def addp(c):
+        E.matmul(out=P[c][:, 0:NPC, :], lhsT=T.ka[:, c, :], rhs=qa, start=False, stop=True).then_inc(sp[c], 1)
 
-    nq = T.lq[:, :, 0, :]
-    E.wait_ge(S.ldkv, 32)
+    E.wait_ge(S.sid, 16)
+    E.wait_ge(S.ldk, 16)
     E.wait_ge(S.cmpo, 2)
     E.wait_ge(S.qbin, nw * len(mates))
-    E.matmul(out=P[ci][:, 0:NPC, :], lhsT=kk(ci), rhs=nq, start=True, stop=True).then_inc(sp[ci], 1)
-    E.matmul(out=T.pa[:, 0:NPC, :], lhsT=vv(ci), rhs=T.lq[:, :, 1 + ci, :], start=True, stop=False)
-    E.wait_ge(kvin[ca], len(off))
-    E.matmul(out=P[ca][:, 0:NPC, :], lhsT=kk(ca), rhs=nq, start=True, stop=True).then_inc(sp[ca], 1)
-    E.matmul(out=T.pa[:, 0:NPC, :], lhsT=vv(ca), rhs=T.lq[:, :, 1 + ca, :], start=False, stop=False)
-    E.wait_ge(sm[ci], 1)
-    E.matmul(out=T.pm[:, 0:NPC, :], lhsT=vv(ci), rhs=T.m[:, ci, :, :], start=True, stop=False)
-    E.wait_ge(kvin[cb], len(off))
-    E.matmul(out=P[cb][:, 0:NPC, :], lhsT=kk(cb), rhs=nq, start=True, stop=True).then_inc(sp[cb], 1)
-    E.matmul(out=T.pa[:, 0:NPC, :], lhsT=vv(cb), rhs=T.lq[:, :, 1 + cb, :], start=False, stop=True).then_inc(S.sa, 1)
-    E.wait_ge(sm[ca], 1)
-    E.matmul(out=T.pm[:, 0:NPC, :], lhsT=vv(ca), rhs=T.m[:, ca, :, :], start=False, stop=False)
-    E.wait_ge(sm[cb], 1)
-    E.matmul(out=T.pm[:, 0:NPC, :], lhsT=vv(cb), rhs=T.m[:, cb, :, :], start=False, stop=True).then_inc(S.smm, 1)
+    addb(ci)
+    addp(ci)
+    addb(ca)
+    addb(cb)
+    E.wait_ge(kin[ca], len(off))
+    addp(ca)
+    E.wait_ge(kin[cb], len(off))
+    addp(cb)
+    E.wait_ge(S.ldv, 16)
+    E.wait_ge(ss[ci], 1)
+    E.matmul(out=T.po[:, 0:NPC, :], lhsT=T.va[:, ci, :], rhs=T.s[:, ci, :, :], start=True, stop=False)
+    E.wait_ge(ss[ca], 1)
+    E.wait_ge(vin[ca], len(off))
+    E.matmul(out=T.po[:, 0:NPC, :], lhsT=T.va[:, ca, :], rhs=T.s[:, ca, :, :], start=False, stop=False)
+    E.wait_ge(ss[cb], 1)
+    E.wait_ge(vin[cb], len(off))
+    E.matmul(out=T.po[:, 0:NPC, :], lhsT=T.va[:, cb, :], rhs=T.s[:, cb, :, :], start=False, stop=True).then_inc(S.spo, 1)
 
     g.sync.wait_ge(S.sy, 1)
     g.sync.dma_start(T.y[:, :], T.ys[:, :]).then_inc(S.sty, 16)

from concourse.bass import DstId, RemoteDMATransfer
from concourse.mybir import AluOpType

NCH = 3
NPC = 4
QP = 32

SCRATCH = {
    "ka": ("sbuf", [128, NCH, 128], "bfloat16"),
    "va": ("sbuf", [128, NCH, 128], "bfloat16"),
    "qs": ("sbuf", [128, QP], "bfloat16"),
    "zero": ("sbuf", [128, NPC, QP], "bfloat16"),
    "z": ("sbuf", [128, 129], "bfloat16"),
    "zd": ("dram", [1, 128 * 129], "bfloat16"),
    "idn": ("sbuf", [128, 128], "bfloat16"),
    "bs": ("sbuf", [128, NCH, NPC, QP], "bfloat16"),
    "win": ("sbuf", [128, NPC, 1 + NCH, QP], "bfloat16"),
    "lq": ("sbuf", [128, NPC, 1 + NCH, QP], "bfloat16"),
    "s": ("sbuf", [128, NCH, NPC, QP], "bfloat16"),
    "ob": ("sbuf", [128, NPC, QP], "bfloat16"),
    "lo": ("sbuf", [128, NPC, QP], "bfloat16"),
    "t": ("sbuf", [128, 2, QP], "float32"),
    "ys": ("sbuf", [128, QP], "bfloat16"),
    "p0": ("psum", [128, 16, QP], "float32"),
    "p1": ("psum", [128, 16, QP], "float32"),
    "p2": ("psum", [128, 16, QP], "float32"),
    "po": ("psum", [128, 16, QP], "float32"),
}
SEMAPHORES = ["ldk", "ldv", "ldq", "ldb", "vz", "vid", "sd1", "sid", "cmpw", "cmpo", "kin0", "kin1", "kin2", "vin0", "vin1",
              "vin2", "qbin", "sp0", "sp1", "sp2", "ss0", "ss1", "ss2", "spo", "so", "oin", "st", "sy", "sty", "sent"]


def _bits(mask):
    return [e for e in range(mask.bit_length()) if (mask >> e) & 1]


def _mask(bits):
    m = 0
    for e in bits:
        m |= 1 << e
    return m


def rank_program(g, core, T, topo):
    rank = T.rank_of(core)
    if rank is None:
        return
    S = T.sem
    cores = list(T.cores)
    chips = []
    for c in cores:
        if topo.chip(c) not in chips:
            chips.append(topo.chip(c))
    groups = [[c for c in cores if topo.chip(c) == ch] for ch in chips]
    ci = chips.index(topo.chip(core))
    oi = groups[ci].index(core)
    assert len(chips) == NCH and all(len(gr) == NPC for gr in groups) and rank == ci * NPC + oi

    def dst_id(c):
        rid, pid, _ = topo.addr(c)
        return DstId(rid=rid, pnc=pid)

    far = [groups[(ci + 1) % NCH][oi], groups[(ci + 2) % NCH][oi]]
    for c in far:
        assert topo.may_write(core, c) and topo.die(c) == topo.die(core)
    ca, cb = (ci - 1) % NCH, (ci + 1) % NCH
    mates = [o for o in range(NPC) if o != oi]

    off = _bits(topo.mask(core, far[0]) & topo.mask(core, far[1]))
    stay = [e for e in _bits(topo.mask(core, groups[ci][mates[0]])) if e not in off]
    nw = 1
    while nw * 2 * len(mates) <= len(stay):
        nw *= 2
    wmask = [stay[i * nw:(i + 1) * nw] for i in range(len(mates))]
    used = off + [e for w in wmask for e in w]
    no = 1
    while no * 2 * len(mates) <= len(used):
        no *= 2
    omask = [used[i * no:(i + 1) * no] for i in range(len(mates))]

    P = [T.p0, T.p1, T.p2]
    sp = [S.sp0, S.sp1, S.sp2]
    ss = [S.ss0, S.ss1, S.ss2]
    kin = [S.kin0, S.kin1, S.kin2]
    vin = [S.vin0, S.vin1, S.vin2]

    g.sync.dma_start(T.ka[:, ci, :], T.k[:, :]).then_inc(S.ldk, 16)
    g.scalar.dma_start(T.va[:, ci, :], T.v[:, :]).then_inc(S.ldv, 16)
    g.sync.dma_start(T.qs[:, :], T.q[:, :]).then_inc(S.ldq, 16)
    g.scalar.dma_start(T.bs[:, :, :, :], T.b[:, :]).then_inc(S.ldb, 16)
    g.sync.wait_ge(S.vid, 2)
    g.sync.dma_start(T.zd[0:1, :], T.z[:, :]).then_inc(S.sd1, 16)
    g.sync.wait_ge(S.sd1, 16)
    g.sync.dma_start(T.idn[:, :], T.zd[0:1, 0:128 * 128]).then_inc(S.sid, 16)

    g.wait_ge(S.ldk, 16)
    g.remote_dma_fused([RemoteDMATransfer(
        dst_ids=[dst_id(c) for c in far], dma_engine_mask=_mask(off), remote_sem=kin[ci],
        srcs=[T.ka[:, ci, :]], dsts=[T.ka[:, ci, :] for _ in far])], local_sem=S.sent)
    g.wait_ge(S.ldv, 16)
    g.wait_ge(S.cmpw, 2 * len(mates))
    g.remote_dma_fused([RemoteDMATransfer(
        dst_ids=[dst_id(c) for c in far], dma_engine_mask=_mask(off), remote_sem=vin[ci],
        srcs=[T.va[:, ci, :]], dsts=[T.va[:, ci, :] for _ in far])] + [RemoteDMATransfer(
            dst_ids=[dst_id(groups[ci][o])], dma_engine_mask=_mask(wmask[i]), remote_sem=S.qbin,
            src=T.win[:, o, :, :], dst=T.lq[:, oi, :, :]) for i, o in enumerate(mates)], local_sem=S.sent)
    g.wait_ge(S.so, 1)
    g.remote_dma_fused([RemoteDMATransfer(
        dst_ids=[dst_id(groups[ci][o])], dma_engine_mask=_mask(omask[i]), remote_sem=S.oin,
        src=T.ob[:, o, :], dst=T.lo[:, oi, :]) for i, o in enumerate(mates)], local_sem=S.sent)
    g.wait_ge(S.sent, 2 * len(off) + len(mates) * (nw + no))

    V = g.vector
    V.memset(T.z[:, 0:1], 1.0).then_inc(S.vid, 1)
    V.memset(T.z[:, 1:129], 0.0).then_inc(S.vid, 1)
    V.memset(T.zero[:, :, :], 0.0).then_inc(S.vz, 1)
    V.wait_ge(S.ldq, 16)
    for o in mates:
        V.tensor_copy(out=T.win[:, o, 0, :], in_=T.qs[:, :]).then_inc(S.cmpw, 1)
    V.tensor_copy(out=T.lq[:, oi, 0, :], in_=T.qs[:, :]).then_inc(S.cmpo, 1)
    V.wait_ge(S.ldb, 16)
    for o in mates:
        V.tensor_copy(out=T.win[:, o, 1:1 + NCH, :], in_=T.bs[:, :, o, :]).then_inc(S.cmpw, 1)
    V.tensor_copy(out=T.lq[:, oi, 1:1 + NCH, :], in_=T.bs[:, :, oi, :]).then_inc(S.cmpo, 1)
    V.wait_ge(S.vz, 1)
    for c in (ci, ca, cb):
        V.wait_ge(sp[c], 1)
        V.tensor_tensor(out=T.s[:, c, :, :], in0=P[c][:, 0:NPC, :], in1=T.zero[:, :, :], op=AluOpType.max).then_inc(ss[c], 1)
    V.wait_ge(S.spo, 1)
    V.tensor_copy(out=T.ob[:, :, :], in_=T.po[:, 0:NPC, :]).then_inc(S.so, 1)
    V.wait_ge(S.so, 1)
    V.wait_ge(S.oin, no * len(mates))
    V.tensor_tensor(out=T.t[:, 0, :], in0=T.lo[:, mates[0], :], in1=T.lo[:, mates[1], :], op=AluOpType.add).then_inc(S.st, 1)
    V.tensor_tensor(out=T.t[:, 1, :], in0=T.lo[:, mates[2], :], in1=T.ob[:, oi, :], op=AluOpType.add).then_inc(S.st, 1)
    V.wait_ge(S.st, 2)
    V.tensor_tensor(out=T.ys[:, :], in0=T.t[:, 0, :], in1=T.t[:, 1, :], op=AluOpType.add).then_inc(S.sy, 1)

    E = g.tensor
    qa = T.lq[:, :, 0, :]

    def addb(c):
        E.matmul(out=P[c][:, 0:NPC, :], lhsT=T.idn[:, :], rhs=T.lq[:, :, 1 + c, :], start=True, stop=False)

    def addp(c):
        E.matmul(out=P[c][:, 0:NPC, :], lhsT=T.ka[:, c, :], rhs=qa, start=False, stop=True).then_inc(sp[c], 1)

    E.wait_ge(S.sid, 16)
    E.wait_ge(S.ldk, 16)
    E.wait_ge(S.cmpo, 2)
    E.wait_ge(S.qbin, nw * len(mates))
    addb(ci)
    addp(ci)
    addb(ca)
    addb(cb)
    E.wait_ge(kin[ca], len(off))
    addp(ca)
    E.wait_ge(kin[cb], len(off))
    addp(cb)
    E.wait_ge(S.ldv, 16)
    E.wait_ge(ss[ci], 1)
    E.matmul(out=T.po[:, 0:NPC, :], lhsT=T.va[:, ci, :], rhs=T.s[:, ci, :, :], start=True, stop=False)
    E.wait_ge(ss[ca], 1)
    E.wait_ge(vin[ca], len(off))
    E.matmul(out=T.po[:, 0:NPC, :], lhsT=T.va[:, ca, :], rhs=T.s[:, ca, :, :], start=False, stop=False)
    E.wait_ge(ss[cb], 1)
    E.wait_ge(vin[cb], len(off))
    E.matmul(out=T.po[:, 0:NPC, :], lhsT=T.va[:, cb, :], rhs=T.s[:, cb, :, :], start=False, stop=True).then_inc(S.spo, 1)

    g.sync.wait_ge(S.sy, 1)
    g.sync.dma_start(T.y[:, :], T.ys[:, :]).then_inc(S.sty, 16)
    g.sync.wait_ge(S.sty, 16)
